import numpy as np
import ml_dtypes


def mxq(x, axis, fmt="e4m3"):
    dtype, down = {"e4m3": (ml_dtypes.float8_e4m3fn, 7), "e5m2": (ml_dtypes.float8_e5m2, 14)}[fmt]
    v = np.moveaxis(np.asarray(x, np.float32).astype(ml_dtypes.bfloat16).astype(np.float64), axis, -1)
    blocks = v.reshape(v.shape[:-1] + (-1, 32))
    amax = np.abs(blocks).max(-1, keepdims=True)
    byte = np.maximum(np.where(amax > 0, np.frexp(amax)[1] - 1 + 127, 0) - down, 1)
    scale = np.exp2(byte - 127.0)
    codes = (blocks / scale).astype(np.float32).astype(dtype).astype(np.float64)
    return np.moveaxis((codes * scale).reshape(v.shape), -1, axis)


WIDE = False


def mx_kscale(k):
    if not WIDE:
        return np.ones(k)
    levels = np.array([10, -10, 5, -5, 0])
    if k % 512:
        return np.exp2(np.random.permutation(np.resize(levels, k // 32))).repeat(32)
    a = np.empty((k // 512, 16))
    for p in range(k // 512):
        a[p, :8] = np.random.permutation(np.resize(levels, 8))
        for g in range(8):
            far = levels[np.abs(levels - a[p, g]) >= 10]
            a[p, g + 8] = far[np.random.randint(len(far))]
    return np.exp2(a.ravel()).repeat(32)


def f64(x):
    return np.asarray(x).astype(np.float64)


def striped(idx):
    return np.tile(idx.reshape(-1, 16).T, (8, 1)).astype(np.uint16)


def unstriped(offs):
    return offs[:16].T.reshape(-1).astype(np.int64)


def striped8(idx):
    return np.concatenate([x.reshape(-1, 16).T for x in idx]).astype(np.uint16)


def runs(offs, k):
    lists = np.stack([offs[16 * r : 16 * r + 16].T.reshape(-1) for r in range(8)]).astype(np.int64)
    return lists[np.arange(k) % 512 // 64]


def pack_weight(w):
    k, n = w.shape
    w = f64(np.asarray(w, np.float32).astype(ml_dtypes.bfloat16)).reshape(k // 32, 32, n)
    amax = np.abs(w).max(1)
    byte = np.clip(np.where(amax > 0, np.frexp(amax)[1] - 1 + 127 - 7, 1), 1, 254)
    scaled = (w * np.exp2(127.0 - byte)[:, None, :]).reshape(k, n).astype(np.float32)
    words = np.ascontiguousarray(scaled.reshape(k // 512, 128, 4, n).transpose(0, 1, 3, 2)).astype(ml_dtypes.float8_e4m3fn).view(np.uint8)
    return words, np.ascontiguousarray(byte.astype(np.uint8).reshape(k // 512, 16, n))


def unpack_weight(words, scales):
    g, p, n, _ = words.shape
    vals = np.ascontiguousarray(words).view(ml_dtypes.float8_e4m3fn).astype(np.float64) * np.repeat(np.exp2(scales.astype(np.float64) - 127.0), 8, axis=1)[..., None]
    return vals.transpose(0, 1, 3, 2).reshape(g * 512, n)


K, T, S, V, N, H = 512, 2048, 1024, 512, 512, 512


def setup_inputs():
    n = np.random.standard_normal
    s = mx_kscale(K)[:, None]
    u = mx_kscale(H)
    packed_xT = pack_weight(n((K, T)) * s)
    return {
        "x_words": packed_xT[0],
        "x_scales": packed_xT[1],
        "w1": (n((K, H)) / np.sqrt(K) / s * u).astype(np.float32),
        "w2": (n((H, H)) / np.sqrt(H) / u[:, None] * u).astype(np.float32),
        "res": (2 * n((N, S))).astype(np.float32),
        "w3": (n((H, N)) / np.sqrt(H) / u[:, None]).astype(np.float32),
        "offs": striped(np.random.permutation(T)[:S]),
        "nb": striped8(np.stack([np.random.permutation(S) for _ in range(8)])),
        "c1": striped8(np.stack([np.random.permutation(S)[:V] for _ in range(8)])),
        "c2": striped8(np.stack([np.random.permutation(S)[:V] for _ in range(8)])),
        "up": striped8(np.random.randint(0, V, (8, S))),
    }


def reference(x_words, x_scales, w1, w2, res, w3, offs, nb, c1, c2, up):
    xq = unpack_weight(x_words, x_scales)[:, unstriped(offs)]
    y = mxq(f64(w1), 0, "e4m3").T @ xq
    rs = y - (y[np.arange(H)[:, None], runs(nb, H)])
    c = rs[np.arange(H)[:, None], runs(c1, H)] + rs[np.arange(H)[:, None], runs(c2, H)]
    h = mxq(f64(w2), 0, "e4m3").T @ mxq(c, 0, "e4m3")
    z2 = rs - (h[np.arange(H)[:, None], runs(up, H)])
    return f64(res) + (mxq(f64(w3), 0, "e4m3").T @ mxq(z2, 0, "e4m3"))

@@ -1,0 +1,220 @@
+from contextlib import ExitStack
+
+import concourse.mybir as mybir
+
+K, T, S, V, H, N = 512, 2048, 1024, 512, 512, 512
+FLOPS = 2 * K * H * S + 2 * H * H * V + 2 * H * N * S
+
+F32 = mybir.dt.float32
+BF16 = mybir.dt.bfloat16
+I32 = mybir.dt.int32
+U32 = mybir.dt.uint32
+U16 = mybir.dt.uint16
+U8 = mybir.dt.uint8
+FP8X4 = mybir.dt.float8_e4m3fn_x4
+ADD = mybir.AluOpType.add
+SUB = mybir.AluOpType.subtract
+
+P = 128
+PACK = 4
+PER_COL = 16
+
+TOKEN_PIECES = ((0, 512), (512, 256), (768, 256))
+COARSE_PIECES = ((0, 256), (256, 256))
+PLACE_PIECES = ((0, 256), (256, 256), (512, 256), (768, 128), (896, 128))
+
+
+def entries(offsets, start, count):
+    return offsets[:, start // PER_COL : (start + count) // PER_COL]
+
+
+def interleave(copy, grouped, planes):
+    copy(
+        out=grouped.rearrange("p (c i t) -> p c t i", i=4, t=PACK),
+        in_=planes.rearrange("p t (c i) -> p c t i", i=4),
+    )
+
+
+def deal(copy, grouped, raw, m0, count):
+    copy(
+        out=grouped.rearrange("p (t m j) -> p m t j", t=PACK, j=PACK)[:, m0 : m0 + count],
+        in_=raw.rearrange("p j (m t) -> p m t j", t=PACK),
+    )
+
+
+def tile_picked_twogrid_none_p_kernel(
+    tc, x_words, x_scales, w1, w2, res, w3, offs, nb, c1, c2, up, out
+):
+    nc = tc.nc
+    with ExitStack() as ctx:
+        lists = ctx.enter_context(tc.tile_pool(name="lists", bufs=1))
+        keep = ctx.enter_context(tc.tile_pool(name="keep", bufs=1))
+        psum = ctx.enter_context(tc.psum_pool(name="psum", bufs=1))
+
+        def quantize(grouped, name):
+            width = grouped.shape[1] // PACK
+            codes = keep.tile([P, width], U32, name=name + "_codes", align_bytes=64)
+            scales = keep.tile([P, width], U8, name=name + "_scales", align_bytes=64)
+            nc.vector.quantize_mx(out=codes[:].bitcast(FP8X4), scales=scales[:], in_=grouped)
+            return codes, scales
+
+        def product(acc, weights, t, moving_codes, moving_scales):
+            cols = slice(t * P, (t + 1) * P)
+            nc.tensor.matmul_mx(
+                out=acc,
+                lhsT=weights[0][:, cols].bitcast(FP8X4),
+                lhsT_scale=weights[1][:, cols],
+                rhs=moving_codes.bitcast(FP8X4),
+                rhs_scale=moving_scales,
+                start=True,
+                stop=True,
+            )
+
+        def load_list(src, name):
+            tile = lists.tile(list(src.shape), U16, name=name)
+            nc.sync.dma_start(tile[:], src)
+            return tile
+
+        scale_table = keep.tile([P, T], U8, align_bytes=64)
+        nc.vector.memset(scale_table[:].bitcast(I32), 0)
+        offs_sb = load_list(offs, "offs_sb")
+        for q in range(4):
+            nc.sync.dma_start(
+                scale_table[32 * q : 32 * q + 4, :].bitcast(I32),
+                x_scales[0, 4 * q : 4 * q + 4, :].bitcast(I32),
+            )
+        w1_raw = []
+        for half in range(2):
+            raw = keep.tile([P, PACK, H // 2], F32, name=f"w1_raw{half}")
+            cols = slice(half * H // 2, (half + 1) * H // 2)
+            nc.sync.dma_start(raw[:], w1[:, cols].rearrange("(p j) c -> p j c", j=PACK))
+            w1_raw.append(raw)
+        word_table = keep.tile([P, T], U32, align_bytes=64)
+        nc.sync.dma_start(word_table[:].bitcast(I32), x_words[0].rearrange("p n r -> p (n r)").bitcast(I32))
+        nb_sb = load_list(nb, "nb_sb")
+        c1_sb = load_list(c1, "c1_sb")
+        c2_sb = load_list(c2, "c2_sb")
+        up_sb = load_list(up, "up_sb")
+        w2_raw = keep.tile([P, PACK, H], F32)
+        nc.sync.dma_start(w2_raw[:], w2.rearrange("(p j) c -> p j c", j=PACK))
+        w3_raw = keep.tile([P, PACK, N], F32)
+        nc.sync.dma_start(w3_raw[:], w3.rearrange("(p j) c -> p j c", j=PACK))
+        res_sb = keep.tile([P, PACK, S], F32)
+        nc.sync.dma_start(res_sb[:], res.rearrange("(t p) s -> p t s", p=P))
+
+        x_scale = keep.tile([P, S], U8, align_bytes=64)
+        nc.vector.tensor_copy(x_scale[:], scale_table[:].indirect(offs_sb[:]))
+        w1_bf = keep.tile([P, PACK * H], BF16, align_bytes=64)
+        deal(nc.scalar.copy, w1_bf[:], w1_raw[0][:], 0, P // 2)
+        deal(nc.vector.tensor_copy, w1_bf[:], w1_raw[1][:], P // 2, P // 2)
+        w1_q = quantize(w1_bf[:], "w1")
+
+        y_acc = {}
+        bank = 0
+        for start, width in TOKEN_PIECES:
+            x_code = keep.tile([P, width], U32, name=f"x_code{start}", align_bytes=64)
+            nc.vector.tensor_copy(x_code[:], word_table[:].indirect(entries(offs_sb, start, width)))
+            share = 512 // width
+            for t in range(PACK):
+                if t % share == 0:
+                    acc = psum.tile([P, share, width], F32, name="acc", tag=f"bank{bank}")
+                    bank = bank + 1
+                product(acc[:, t % share, :], w1_q, t, x_code[:], x_scale[:, start : start + width])
+                y_acc[start, t] = acc[:, t % share, :]
+
+        y_neg = [keep.tile([P, S], F32, name=f"y_neg{t}") for t in range(PACK)]
+        y_pos = [keep.tile([P, S], F32, name=f"y_pos{t}") for t in range(PACK)]
+        rs = [keep.tile([P, S], F32, name=f"rs{t}") for t in range(PACK)]
+        c_first = [keep.tile([P, V], F32, name=f"c_first{t}") for t in range(PACK)]
+        c_sum = [keep.tile([P, PACK, width], F32, name=f"c_sum{start}") for start, width in COARSE_PIECES]
+
+        def first_residual(t):
+            (start, width) = TOKEN_PIECES[0]
+            nc.scalar.copy(y_neg[t][:, start : start + width], y_acc[start, t])
+            nc.scalar.copy(y_pos[t][:, start : start + width], y_acc[start, t])
+            for start, width in TOKEN_PIECES[1:]:
+                nc.scalar.copy(y_neg[t][:, start : start + width], y_acc[start, t])
+            for start, width in TOKEN_PIECES[1:]:
+                nc.scalar.copy(y_pos[t][:, start : start + width], y_acc[start, t])
+            for start in (0, 512):
+                cols = slice(start, start + 512)
+                nc.vector.tensor_tensor(
+                    rs[t][:, cols], y_neg[t][:].indirect(entries(nb_sb, start, 512)), y_pos[t][:, cols], SUB
+                )
+
+        def coarse_first(t):
+            nc.vector.tensor_copy(c_first[t][:], rs[t][:].indirect(c1_sb[:]))
+
+        def coarse_sum(piece, t):
+            start, width = COARSE_PIECES[piece]
+            nc.vector.tensor_tensor(
+                c_sum[piece][:, t, :],
+                rs[t][:].indirect(entries(c2_sb, start, width)),
+                c_first[t][:, start : start + width],
+                ADD,
+            )
+
+        for t in range(PACK):
+            first_residual(t)
+            if t > 0:
+                coarse_first(t - 1)
+            if t > 1:
+                coarse_sum(0, t - 2)
+
+        w2_bf = keep.tile([P, PACK * H], BF16, align_bytes=64)
+        deal(nc.scalar.copy, w2_bf[:], w2_raw[:], 0, P)
+        w2_q = quantize(w2_bf[:], "w2")
+        coarse_first(PACK - 1)
+        coarse_sum(0, PACK - 2)
+        coarse_sum(0, PACK - 1)
+
+        h_neg = [keep.tile([P, V], F32, name=f"h_neg{t}") for t in range(PACK)]
+
+        def coarse_product(piece, c_q, banks):
+            start, width = COARSE_PIECES[piece]
+            for t in range(PACK):
+                acc = psum.tile([P, width], F32, name="acc", tag=f"bank{banks + t}")
+                product(acc[:], w2_q, t, c_q[0][:], c_q[1][:])
+                nc.scalar.copy(h_neg[t][:, start : start + width], acc[:])
+
+        c_bf0 = keep.tile([P, PACK * 256], BF16, align_bytes=64)
+        interleave(nc.scalar.copy, c_bf0[:], c_sum[0][:])
+        w3_bf = keep.tile([P, PACK * N], BF16, align_bytes=64)
+        coarse_sum(1, 0)
+        coarse_sum(1, 1)
+        coarse_sum(1, 2)
+        c_q0 = quantize(c_bf0[:], "c0")
+        coarse_product(0, c_q0, 0)
+        coarse_sum(1, 3)
+        interleave(nc.scalar.copy, w3_bf[:], w3_raw[:])
+        c_bf1 = keep.tile([P, PACK * 256], BF16, align_bytes=64)
+        split = 160
+        interleave(nc.vector.tensor_copy, c_bf1[:, : PACK * split], c_sum[1][:, :, :split])
+        interleave(nc.scalar.copy, c_bf1[:, PACK * split :], c_sum[1][:, :, split:])
+        c_q1 = quantize(c_bf1[:], "c1")
+        coarse_product(1, c_q1, 4)
+        w3_q = quantize(w3_bf[:], "w3")
+
+        out_rows = out.rearrange("(t p) s -> p t s", p=P)
+        bank = 0
+        for piece, (start, width) in enumerate(PLACE_PIECES):
+            cols = slice(start, start + width)
+            z = keep.tile([P, PACK, width], F32, name=f"z{piece}")
+            for t in range(PACK):
+                nc.vector.tensor_tensor(
+                    z[:, t, :], h_neg[t][:].indirect(entries(up_sb, start, width)), rs[t][:, cols], SUB
+                )
+            z_bf = keep.tile([P, PACK * width], BF16, name=f"z_bf{piece}", align_bytes=64)
+            last = piece == len(PLACE_PIECES) - 1
+            interleave(nc.vector.tensor_copy if last else nc.scalar.copy, z_bf[:], z[:])
+            z_q = quantize(z_bf[:], f"z{piece}")
+            result = keep.tile([P, PACK, width], F32, name=f"result{piece}")
+            share = 512 // width
+            for first in range(0, PACK, share):
+                acc = psum.tile([P, share, width], F32, name="acc", tag=f"bank{bank}")
+                bank = bank + 1
+                for t in range(first, first + share):
+                    product(acc[:, t - first, :], w3_q, t, z_q[0][:], z_q[1][:])
+                rows = slice(first, first + share)
+                nc.vector.tensor_tensor(result[:, rows, :], acc[:], res_sb[:, rows, cols], ADD)
+            nc.sync.dma_start(out_rows[:, :, cols], result[:])

@@ -1,6 +1,7 @@
 from contextlib import ExitStack
 
 import concourse.mybir as mybir
+from concourse.masks import make_identity
 
 K, T, S, V, H, N = 512, 2048, 1024, 512, 512, 512
 FLOPS = 2 * K * H * S + 2 * H * H * V + 2 * H * N * S
@@ -18,10 +19,12 @@ SUB = mybir.AluOpType.subtract
 P = 128
 PACK = 4
 PER_COL = 16
+BANK = 512
 
 TOKEN_PIECES = ((0, 512), (512, 256), (768, 256))
-COARSE_PIECES = ((0, 256), (256, 256))
+HALF = V // 2
 PLACE_PIECES = ((0, 256), (256, 256), (512, 256), (768, 128), (896, 128))
+TURNED = 512
 
 
 def entries(offsets, start, count):
@@ -51,24 +54,26 @@ def tile_picked_twogrid_none_p_kernel(
         keep = ctx.enter_context(tc.tile_pool(name="keep", bufs=1))
         psum = ctx.enter_context(tc.psum_pool(name="psum", bufs=1))
 
-        def quantize(grouped, name):
+        def quantize(grouped, name, tag=""):
             width = grouped.shape[1] // PACK
-            codes = keep.tile([P, width], U32, name=name + "_codes", align_bytes=64)
+            codes = keep.tile([P, width], U32, name=name + "_codes", tag=tag, align_bytes=64)
             scales = keep.tile([P, width], U8, name=name + "_scales", align_bytes=64)
             nc.vector.quantize_mx(out=codes[:].bitcast(FP8X4), scales=scales[:], in_=grouped)
             return codes, scales
 
-        def product(acc, weights, t, moving_codes, moving_scales):
-            cols = slice(t * P, (t + 1) * P)
+        def product(acc, still, cols, moving_codes, moving_scales):
             nc.tensor.matmul_mx(
                 out=acc,
-                lhsT=weights[0][:, cols].bitcast(FP8X4),
-                lhsT_scale=weights[1][:, cols],
+                lhsT=still[0][:, cols].bitcast(FP8X4),
+                lhsT_scale=still[1][:, cols],
                 rhs=moving_codes.bitcast(FP8X4),
                 rhs_scale=moving_scales,
                 start=True,
                 stop=True,
             )
+
+        def block(t):
+            return slice(t * P, (t + 1) * P)
 
         def load_list(src, name):
             tile = lists.tile(list(src.shape), U16, name=name)
@@ -76,7 +81,7 @@ def tile_picked_twogrid_none_p_kernel(
             return tile
 
         scale_table = keep.tile([P, T], U8, align_bytes=64)
-        nc.vector.memset(scale_table[:].bitcast(I32), 0)
+        nc.gpsimd.memset(scale_table[:].bitcast(I32), 0)
         offs_sb = load_list(offs, "offs_sb")
         for q in range(4):
             nc.sync.dma_start(
@@ -97,10 +102,15 @@ def tile_picked_twogrid_none_p_kernel(
         up_sb = load_list(up, "up_sb")
         w2_raw = keep.tile([P, PACK, H], F32)
         nc.sync.dma_start(w2_raw[:], w2.rearrange("(p j) c -> p j c", j=PACK))
+        res_rows = res.rearrange("(t p) s -> p t s", p=P)
+        res_head = keep.tile([P, PACK, TURNED], F32)
+        nc.sync.dma_start(res_head[:], res_rows[:, :, :TURNED])
         w3_raw = keep.tile([P, PACK, N], F32)
         nc.sync.dma_start(w3_raw[:], w3.rearrange("(p j) c -> p j c", j=PACK))
-        res_sb = keep.tile([P, PACK, S], F32)
-        nc.sync.dma_start(res_sb[:], res.rearrange("(t p) s -> p t s", p=P))
+        res_tail = keep.tile([P, PACK, S - TURNED], F32)
+        nc.sync.dma_start(res_tail[:], res_rows[:, :, TURNED:])
+        identity = keep.tile([P, P], F32)
+        make_identity(nc, identity[:])
 
         x_scale = keep.tile([P, S], U8, align_bytes=64)
         nc.vector.tensor_copy(x_scale[:], scale_table[:].indirect(offs_sb[:]))
@@ -109,112 +119,173 @@ def tile_picked_twogrid_none_p_kernel(
         deal(nc.vector.tensor_copy, w1_bf[:], w1_raw[1][:], P // 2, P // 2)
         w1_q = quantize(w1_bf[:], "w1")
 
-        y_acc = {}
-        bank = 0
+        x_code = []
         for start, width in TOKEN_PIECES:
-            x_code = keep.tile([P, width], U32, name=f"x_code{start}", align_bytes=64)
-            nc.vector.tensor_copy(x_code[:], word_table[:].indirect(entries(offs_sb, start, width)))
-            share = 512 // width
-            for t in range(PACK):
-                if t % share == 0:
-                    acc = psum.tile([P, share, width], F32, name="acc", tag=f"bank{bank}")
-                    bank = bank + 1
-                product(acc[:, t % share, :], w1_q, t, x_code[:], x_scale[:, start : start + width])
-                y_acc[start, t] = acc[:, t % share, :]
+            piece_code = keep.tile([P, width], U32, name=f"x_code{start}", align_bytes=64)
+            nc.vector.tensor_copy(piece_code[:], word_table[:].indirect(entries(offs_sb, start, width)))
+            x_code.append(piece_code)
+        narrow = {
+            (piece, parity): psum.tile([P, 2, 256], F32, name="acc", tag=f"bank{2 + 2 * piece + parity}")
+            for piece in (1, 2)
+            for parity in (0, 1)
+        }
 
-        y_neg = [keep.tile([P, S], F32, name=f"y_neg{t}") for t in range(PACK)]
-        y_pos = [keep.tile([P, S], F32, name=f"y_pos{t}") for t in range(PACK)]
-        rs = [keep.tile([P, S], F32, name=f"rs{t}") for t in range(PACK)]
-        c_first = [keep.tile([P, V], F32, name=f"c_first{t}") for t in range(PACK)]
-        c_sum = [keep.tile([P, PACK, width], F32, name=f"c_sum{start}") for start, width in COARSE_PIECES]
+        y_win = [keep.tile([P, S], F32, name=f"y_win{t}", align_bytes=64) for t in range(PACK)]
+        y_own = [[keep.tile([P, S // 2], F32, name=f"y_own{t}_{half}", align_bytes=64) for half in range(2)] for t in range(PACK)]
+        d = [keep.tile([P, S], F32, name=f"d{t}") for t in range(PACK)]
+        c_first = {}
+        c_sum = {}
 
-        def first_residual(t):
+        def fine_residual(t):
+            y_acc = {}
+            for piece, (start, width) in enumerate(TOKEN_PIECES):
+                if piece == 0:
+                    acc = psum.tile([P, BANK], F32, name="acc", tag=f"bank{t}")[:]
+                else:
+                    acc = narrow[piece, t % 2][:, t // 2, :]
+                product(acc, w1_q, block(t), x_code[piece][:], x_scale[:, start : start + width])
+                y_acc[start, t] = acc
             (start, width) = TOKEN_PIECES[0]
-            nc.scalar.copy(y_neg[t][:, start : start + width], y_acc[start, t])
-            nc.scalar.copy(y_pos[t][:, start : start + width], y_acc[start, t])
+            nc.scalar.copy(y_win[t][:, start : start + width], y_acc[start, t])
+            own_copy = nc.vector.tensor_copy if t == 0 else nc.scalar.copy
+            own_copy(y_own[t][0][:], y_acc[start, t])
             for start, width in TOKEN_PIECES[1:]:
-                nc.scalar.copy(y_neg[t][:, start : start + width], y_acc[start, t])
+                nc.scalar.copy(y_win[t][:, start : start + width], y_acc[start, t])
             for start, width in TOKEN_PIECES[1:]:
-                nc.scalar.copy(y_pos[t][:, start : start + width], y_acc[start, t])
-            for start in (0, 512):
-                cols = slice(start, start + 512)
+                nc.scalar.copy(y_own[t][1][:, start - S // 2 : start - S // 2 + width], y_acc[start, t])
+            for start in (0, S // 2):
+                cols = slice(start, start + S // 2)
                 nc.vector.tensor_tensor(
-                    rs[t][:, cols], y_neg[t][:].indirect(entries(nb_sb, start, 512)), y_pos[t][:, cols], SUB
+                    d[t][:, cols], y_win[t][:].indirect(entries(nb_sb, start, S // 2)), y_own[t][start // (S // 2)][:], SUB
                 )
 
-        def coarse_first(t):
-            nc.vector.tensor_copy(c_first[t][:], rs[t][:].indirect(c1_sb[:]))
+        def coarse_first(t, start, width):
+            nc.vector.tensor_copy(c_first[t][:, start : start + width], d[t][:].indirect(entries(c1_sb, start, width)))
 
-        def coarse_sum(piece, t):
-            start, width = COARSE_PIECES[piece]
+        def coarse_sum(half, t):
             nc.vector.tensor_tensor(
-                c_sum[piece][:, t, :],
-                rs[t][:].indirect(entries(c2_sb, start, width)),
-                c_first[t][:, start : start + width],
+                c_sum[half][:, t * HALF : (t + 1) * HALF],
+                d[t][:].indirect(entries(c2_sb, half * HALF, HALF)),
+                c_first[t][:, half * HALF : (half + 1) * HALF],
                 ADD,
             )
 
         for t in range(PACK):
-            first_residual(t)
+            fine_residual(t)
             if t > 0:
-                coarse_first(t - 1)
-            if t > 1:
-                coarse_sum(0, t - 2)
+                c_first[t - 1] = keep.tile([P, V], F32, name="c_first", tag=f"y_own{t}_0", align_bytes=64)
+                coarse_first(t - 1, 0, V)
 
-        w2_bf = keep.tile([P, PACK * H], BF16, align_bytes=64)
+        w2_bf = keep.tile([P, PACK * H], BF16, tag="y_win1", align_bytes=64)
         deal(nc.scalar.copy, w2_bf[:], w2_raw[:], 0, P)
         w2_q = quantize(w2_bf[:], "w2")
-        coarse_first(PACK - 1)
-        coarse_sum(0, PACK - 2)
-        coarse_sum(0, PACK - 1)
+        w3_bf = keep.tile([P, PACK * N], BF16, tag="y_win2", align_bytes=64)
+        interleave(nc.scalar.copy, w3_bf[:], w3_raw[:])
 
-        h_neg = [keep.tile([P, V], F32, name=f"h_neg{t}") for t in range(PACK)]
-
-        def coarse_product(piece, c_q, banks):
-            start, width = COARSE_PIECES[piece]
+        total = []
+        for b in range(TURNED // P):
+            acc = psum.tile([P, N], F32, name="acc", tag=f"bank{4 + b}")
             for t in range(PACK):
-                acc = psum.tile([P, width], F32, name="acc", tag=f"bank{banks + t}")
-                product(acc[:], w2_q, t, c_q[0][:], c_q[1][:])
-                nc.scalar.copy(h_neg[t][:, start : start + width], acc[:])
+                nc.tensor.transpose(acc[:, block(t)], res_head[:, t, block(b)], identity[:])
+            turned = keep.tile([P, N], F32, name=f"res_turned{b}")
+            nc.scalar.copy(turned[:], acc[:])
+            total.append(psum.tile([P, PACK, P], F32, name="total", tag=f"bank{b}"))
+            for t in range(PACK):
+                nc.tensor.matmul(
+                    total[b][:, t, :], turned[:, block(t)], identity[:], start=t == 0, stop=False, is_transpose=True
+                )
 
-        c_bf0 = keep.tile([P, PACK * 256], BF16, align_bytes=64)
-        interleave(nc.scalar.copy, c_bf0[:], c_sum[0][:])
-        w3_bf = keep.tile([P, PACK * N], BF16, align_bytes=64)
+        c_first[PACK - 1] = keep.tile([P, V], F32, name="c_last")
+        c_both = keep.tile([P, (2 * PACK - 1) * HALF], F32, tag="y_win3", align_bytes=64)
+        c_sum[0] = c_both[:, (PACK - 1) * HALF :]
+        c_sum[1] = c_both[:, : PACK * HALF]
+        coarse_first(PACK - 1, 0, HALF)
+        for t in range(PACK):
+            coarse_sum(0, t)
+        coarse_first(PACK - 1, HALF, HALF)
+
+        h = [keep.tile([P, V], F32, name=f"h{t}") for t in range(PACK)]
+
+        def planes(tile):
+            return tile[:, : PACK * HALF].rearrange("p (t c) -> p t c", t=PACK)
+
+        c_bf0 = keep.tile([P, PACK * HALF], BF16, align_bytes=64)
+        interleave(nc.scalar.copy, c_bf0[:], planes(c_sum[0]))
         coarse_sum(1, 0)
         coarse_sum(1, 1)
         coarse_sum(1, 2)
         c_q0 = quantize(c_bf0[:], "c0")
-        coarse_product(0, c_q0, 0)
+        for first in (0, 2):
+            acc = psum.tile([P, 2, HALF], F32, name="acc", tag=f"bank{4 + first // 2}")
+            for t in (first, first + 1):
+                product(acc[:, t - first, :], w2_q, block(t), c_q0[0][:], c_q0[1][:])
+            for t in (first, first + 1):
+                nc.scalar.copy(h[t][:, :HALF], acc[:, t - first, :])
         coarse_sum(1, 3)
-        interleave(nc.scalar.copy, w3_bf[:], w3_raw[:])
-        c_bf1 = keep.tile([P, PACK * 256], BF16, align_bytes=64)
-        split = 160
-        interleave(nc.vector.tensor_copy, c_bf1[:, : PACK * split], c_sum[1][:, :, :split])
-        interleave(nc.scalar.copy, c_bf1[:, PACK * split :], c_sum[1][:, :, split:])
+        c_bf1 = keep.tile([P, PACK * HALF], BF16, align_bytes=64)
+        interleave(nc.vector.tensor_copy, c_bf1[:], planes(c_sum[1]))
         c_q1 = quantize(c_bf1[:], "c1")
-        coarse_product(1, c_q1, 4)
-        w3_q = quantize(w3_bf[:], "w3")
+        for t in range(PACK):
+            acc = psum.tile([P, HALF], F32, name="acc", tag=f"bank{4 + (t + 2) % 4}")
+            product(acc[:], w2_q, block(t), c_q1[0][:], c_q1[1][:])
+            nc.scalar.copy(h[t][:, HALF:], acc[:])
+        w3_q = quantize(w3_bf[:], "w3", tag="c_bf1")
 
         out_rows = out.rearrange("(t p) s -> p t s", p=P)
-        bank = 0
-        for piece, (start, width) in enumerate(PLACE_PIECES):
-            cols = slice(start, start + width)
-            z = keep.tile([P, PACK, width], F32, name=f"z{piece}")
+        last = len(PLACE_PIECES) - 1
+        z_bf = {}
+
+        def correct(piece):
+            start, width = PLACE_PIECES[piece]
+            z = keep.tile([P, PACK, width], F32, name="z", bufs=2)
             for t in range(PACK):
                 nc.vector.tensor_tensor(
-                    z[:, t, :], h_neg[t][:].indirect(entries(up_sb, start, width)), rs[t][:, cols], SUB
+                    z[:, t, :], h[t][:].indirect(entries(up_sb, start, width)), d[t][:, start : start + width], SUB
                 )
-            z_bf = keep.tile([P, PACK * width], BF16, name=f"z_bf{piece}", align_bytes=64)
-            last = piece == len(PLACE_PIECES) - 1
-            interleave(nc.vector.tensor_copy if last else nc.scalar.copy, z_bf[:], z[:])
-            z_q = quantize(z_bf[:], f"z{piece}")
-            result = keep.tile([P, PACK, width], F32, name=f"result{piece}")
-            share = 512 // width
+            z_bf[piece] = keep.tile([P, PACK * width], BF16, name=f"z_bf{piece}", align_bytes=64)
+            interleave(nc.vector.tensor_copy if piece == last else nc.scalar.copy, z_bf[piece][:], z[:])
+
+        def finish_turned(start, width, z_q):
+            product_turned = []
+            for local in range(width // P):
+                acc = psum.tile([P, N], F32, name="acc", tag=f"bank{4 + local}")
+                product(acc[:], z_q, block(local), w3_q[0][:], w3_q[1][:])
+                product_turned.append(keep.tile([P, N], F32, name="product_turned", bufs=4))
+                nc.scalar.copy(product_turned[local][:], acc[:])
+            for local in range(width // P):
+                b = start // P + local
+                for t in range(PACK):
+                    nc.tensor.matmul(
+                        total[b][:, t, :], product_turned[local][:, block(t)], identity[:],
+                        start=False, stop=t == PACK - 1, is_transpose=True,
+                    )
+                result = keep.tile([P, PACK, P], F32, name=f"result{b}")
+                nc.scalar.copy(result[:], total[b][:])
+                nc.sync.dma_start(out_rows[:, :, block(b)], result[:])
+
+        def finish_direct(piece, start, width, z_q):
+            share = BANK // width
             for first in range(0, PACK, share):
-                acc = psum.tile([P, share, width], F32, name="acc", tag=f"bank{bank}")
-                bank = bank + 1
+                acc = psum.tile([P, share, width], F32, name="acc", tag=f"bank{6 + (piece + first // share) % 2}")
                 for t in range(first, first + share):
-                    product(acc[:, t - first, :], w3_q, t, z_q[0][:], z_q[1][:])
+                    product(acc[:, t - first, :], w3_q, block(t), z_q[0][:], z_q[1][:])
                 rows = slice(first, first + share)
-                nc.vector.tensor_tensor(result[:, rows, :], acc[:], res_sb[:, rows, cols], ADD)
-            nc.sync.dma_start(out_rows[:, :, cols], result[:])
+                result = keep.tile([P, share, width], F32, name=f"result{piece}_{first}")
+                nc.vector.tensor_tensor(
+                    result[:], acc[:], res_tail[:, rows, start - TURNED : start - TURNED + width], ADD
+                )
+                nc.sync.dma_start(out_rows[:, rows, start : start + width], result[:])
+
+        def finish(piece):
+            start, width = PLACE_PIECES[piece]
+            z_q = quantize(z_bf[piece][:], f"z{piece}")
+            if start < TURNED:
+                finish_turned(start, width, z_q)
+            else:
+                finish_direct(piece, start, width, z_q)
+
+        for piece in range(last + 2):
+            if piece <= last:
+                correct(piece)
+            if piece > 0:
+                finish(piece - 1)

@@ -41,7 +41,7 @@ def interleave(copy, grouped, planes):
 def deal(copy, grouped, raw, m0, count):
     copy(
         out=grouped.rearrange("p (t m j) -> p m t j", t=PACK, j=PACK)[:, m0 : m0 + count],
-        in_=raw.rearrange("p j (m t) -> p m t j", t=PACK),
+        in_=raw.rearrange("p j (m t) -> p m t j", t=PACK)[:, m0 : m0 + count],
     )
 
 
@@ -83,20 +83,16 @@ def tile_picked_twogrid_none_p_kernel(
         scale_table = keep.tile([P, T], U8, align_bytes=64)
         nc.gpsimd.memset(scale_table[:].bitcast(I32), 0)
         offs_sb = load_list(offs, "offs_sb")
+        nb_sb = load_list(nb, "nb_sb")
         for q in range(4):
             nc.sync.dma_start(
                 scale_table[32 * q : 32 * q + 4, :].bitcast(I32),
                 x_scales[0, 4 * q : 4 * q + 4, :].bitcast(I32),
             )
-        w1_raw = []
-        for half in range(2):
-            raw = keep.tile([P, PACK, H // 2], F32, name=f"w1_raw{half}")
-            cols = slice(half * H // 2, (half + 1) * H // 2)
-            nc.sync.dma_start(raw[:], w1[:, cols].rearrange("(p j) c -> p j c", j=PACK))
-            w1_raw.append(raw)
+        w1_raw = keep.tile([P, PACK, H], F32)
+        nc.sync.dma_start(w1_raw[:], w1.rearrange("(p j) c -> p j c", j=PACK))
         word_table = keep.tile([P, T], U32, align_bytes=64)
         nc.sync.dma_start(word_table[:].bitcast(I32), x_words[0].rearrange("p n r -> p (n r)").bitcast(I32))
-        nb_sb = load_list(nb, "nb_sb")
         c1_sb = load_list(c1, "c1_sb")
         c2_sb = load_list(c2, "c2_sb")
         up_sb = load_list(up, "up_sb")
@@ -115,20 +111,16 @@ def tile_picked_twogrid_none_p_kernel(
         x_scale = keep.tile([P, S], U8, align_bytes=64)
         nc.vector.tensor_copy(x_scale[:], scale_table[:].indirect(offs_sb[:]))
         w1_bf = keep.tile([P, PACK * H], BF16, align_bytes=64)
-        deal(nc.scalar.copy, w1_bf[:], w1_raw[0][:], 0, P // 2)
-        deal(nc.vector.tensor_copy, w1_bf[:], w1_raw[1][:], P // 2, P // 2)
+        deal(nc.scalar.copy, w1_bf[:], w1_raw[:], 0, 48)
+        deal(nc.vector.tensor_copy, w1_bf[:], w1_raw[:], 48, P - 48)
         w1_q = quantize(w1_bf[:], "w1")
 
-        x_code = []
+        x_code = [keep.tile([P, BANK], U32, name=f"x_code{half}", align_bytes=64) for half in range(2)]
         for start, width in TOKEN_PIECES:
-            piece_code = keep.tile([P, width], U32, name=f"x_code{start}", align_bytes=64)
-            nc.vector.tensor_copy(piece_code[:], word_table[:].indirect(entries(offs_sb, start, width)))
-            x_code.append(piece_code)
-        narrow = {
-            (piece, parity): psum.tile([P, 2, 256], F32, name="acc", tag=f"bank{2 + 2 * piece + parity}")
-            for piece in (1, 2)
-            for parity in (0, 1)
-        }
+            at = start % BANK
+            nc.vector.tensor_copy(
+                x_code[start // BANK][:, at : at + width], word_table[:].indirect(entries(offs_sb, start, width))
+            )
 
         y_win = [keep.tile([P, S], F32, name=f"y_win{t}", align_bytes=64) for t in range(PACK)]
         y_own = [[keep.tile([P, S // 2], F32, name=f"y_own{t}_{half}", align_bytes=64) for half in range(2)] for t in range(PACK)]
@@ -137,22 +129,20 @@ def tile_picked_twogrid_none_p_kernel(
         c_sum = {}
 
         def fine_residual(t):
-            y_acc = {}
-            for piece, (start, width) in enumerate(TOKEN_PIECES):
-                if piece == 0:
-                    acc = psum.tile([P, BANK], F32, name="acc", tag=f"bank{t}")[:]
-                else:
-                    acc = narrow[piece, t % 2][:, t // 2, :]
-                product(acc, w1_q, block(t), x_code[piece][:], x_scale[:, start : start + width])
-                y_acc[start, t] = acc
-            (start, width) = TOKEN_PIECES[0]
-            nc.scalar.copy(y_win[t][:, start : start + width], y_acc[start, t])
-            own_copy = nc.vector.tensor_copy if t == 0 else nc.scalar.copy
-            own_copy(y_own[t][0][:], y_acc[start, t])
-            for start, width in TOKEN_PIECES[1:]:
-                nc.scalar.copy(y_win[t][:, start : start + width], y_acc[start, t])
-            for start, width in TOKEN_PIECES[1:]:
-                nc.scalar.copy(y_own[t][1][:, start - S // 2 : start - S // 2 + width], y_acc[start, t])
+            pieces = TOKEN_PIECES if t == 0 else ((0, BANK), (BANK, BANK))
+            first_bank = (0, 3, 5, 7)[t]
+            y_acc = []
+            for piece, (start, width) in enumerate(pieces):
+                acc = psum.tile([P, width], F32, name="acc", tag=f"bank{(first_bank + piece) % 8}")
+                at = start % BANK
+                product(acc[:], w1_q, block(t), x_code[start // BANK][:, at : at + width], x_scale[:, start : start + width])
+                y_acc.append(acc)
+            for acc, (start, width) in zip(y_acc, pieces):
+                nc.scalar.copy(y_win[t][:, start : start + width], acc[:])
+            for acc, (start, width) in zip(y_acc, pieces):
+                at = start % BANK
+                own_copy = nc.vector.tensor_copy if (t, start) == (0, 0) else nc.scalar.copy
+                own_copy(y_own[t][start // BANK][:, at : at + width], acc[:])
             for start in (0, S // 2):
                 cols = slice(start, start + S // 2)
                 nc.vector.tensor_tensor(

@@ -19,10 +19,11 @@ SUB = mybir.AluOpType.subtract
 P = 128
 PACK = 4
 PER_COL = 16
+QUADRANT = 32
 BANK = 512
-
-TOKEN_PIECES = ((0, 512), (512, 256), (768, 256))
+LINE = 4
 HALF = V // 2
+
 PLACE_PIECES = ((0, 256), (256, 256), (512, 256), (768, 128), (896, 128))
 TURNED = 512
 
@@ -31,17 +32,21 @@ def entries(offsets, start, count):
     return offsets[:, start // PER_COL : (start + count) // PER_COL]
 
 
+def block(index):
+    return slice(index * P, (index + 1) * P)
+
+
 def interleave(copy, grouped, planes):
     copy(
-        out=grouped.rearrange("p (c i t) -> p c t i", i=4, t=PACK),
-        in_=planes.rearrange("p t (c i) -> p c t i", i=4),
+        out=grouped.rearrange("p (c i t) -> p c t i", i=LINE, t=PACK),
+        in_=planes.rearrange("p t (c i) -> p c t i", i=LINE),
     )
 
 
-def deal(copy, grouped, raw, m0, count):
-    copy(
+def deal(nc, grouped, raw, m0, count):
+    nc.scalar.copy(
         out=grouped.rearrange("p (t m j) -> p m t j", t=PACK, j=PACK)[:, m0 : m0 + count],
-        in_=raw.rearrange("p j (m t) -> p m t j", t=PACK)[:, m0 : m0 + count],
+        in_=raw.rearrange("p j (m t) -> p m t j", t=PACK),
     )
 
 
@@ -61,19 +66,16 @@ def tile_picked_twogrid_none_p_kernel(
             nc.vector.quantize_mx(out=codes[:].bitcast(FP8X4), scales=scales[:], in_=grouped)
             return codes, scales
 
-        def product(acc, still, cols, moving_codes, moving_scales):
+        def product(acc, stationary, cols, moving_codes, moving_scales):
             nc.tensor.matmul_mx(
                 out=acc,
-                lhsT=still[0][:, cols].bitcast(FP8X4),
-                lhsT_scale=still[1][:, cols],
+                lhsT=stationary[0][:, cols].bitcast(FP8X4),
+                lhsT_scale=stationary[1][:, cols],
                 rhs=moving_codes.bitcast(FP8X4),
                 rhs_scale=moving_scales,
                 start=True,
                 stop=True,
             )
-
-        def block(t):
-            return slice(t * P, (t + 1) * P)
 
         def load_list(src, name):
             tile = lists.tile(list(src.shape), U16, name=name)
@@ -83,22 +85,26 @@ def tile_picked_twogrid_none_p_kernel(
         scale_table = keep.tile([P, T], U8, align_bytes=64)
         nc.gpsimd.memset(scale_table[:].bitcast(I32), 0)
         offs_sb = load_list(offs, "offs_sb")
-        nb_sb = load_list(nb, "nb_sb")
-        for q in range(4):
+        for q in range(P // QUADRANT):
             nc.sync.dma_start(
-                scale_table[32 * q : 32 * q + 4, :].bitcast(I32),
+                scale_table[QUADRANT * q : QUADRANT * q + 4, :].bitcast(I32),
                 x_scales[0, 4 * q : 4 * q + 4, :].bitcast(I32),
             )
-        w1_raw = keep.tile([P, PACK, H], F32)
-        nc.sync.dma_start(w1_raw[:], w1.rearrange("(p j) c -> p j c", j=PACK))
+        w1_rows = w1.rearrange("(p j) c -> p j c", j=PACK)
+        w1_left = keep.tile([P, PACK, H // 2], F32)
+        nc.sync.dma_start(w1_left[:], w1_rows[:, :, : H // 2])
         word_table = keep.tile([P, T], U32, align_bytes=64)
         nc.sync.dma_start(word_table[:].bitcast(I32), x_words[0].rearrange("p n r -> p (n r)").bitcast(I32))
+        w1_right = keep.tile([P, PACK, H // 2], F32)
+        nc.sync.dma_start(w1_right[:], w1_rows[:, :, H // 2 :])
+        nb_sb = load_list(nb, "nb_sb")
         c1_sb = load_list(c1, "c1_sb")
         c2_sb = load_list(c2, "c2_sb")
         up_sb = load_list(up, "up_sb")
         w2_raw = keep.tile([P, PACK, H], F32)
         nc.sync.dma_start(w2_raw[:], w2.rearrange("(p j) c -> p j c", j=PACK))
         res_rows = res.rearrange("(t p) s -> p t s", p=P)
+        out_rows = out.rearrange("(t p) s -> p t s", p=P)
         res_head = keep.tile([P, PACK, TURNED], F32)
         nc.sync.dma_start(res_head[:], res_rows[:, :, :TURNED])
         w3_raw = keep.tile([P, PACK, N], F32)
@@ -111,158 +117,149 @@ def tile_picked_twogrid_none_p_kernel(
         x_scale = keep.tile([P, S], U8, align_bytes=64)
         nc.vector.tensor_copy(x_scale[:], scale_table[:].indirect(offs_sb[:]))
         w1_bf = keep.tile([P, PACK * H], BF16, align_bytes=64)
-        deal(nc.scalar.copy, w1_bf[:], w1_raw[:], 0, 48)
-        deal(nc.vector.tensor_copy, w1_bf[:], w1_raw[:], 48, P - 48)
-        w1_q = quantize(w1_bf[:], "w1")
-
-        x_code = [keep.tile([P, BANK], U32, name=f"x_code{half}", align_bytes=64) for half in range(2)]
-        for start, width in TOKEN_PIECES:
-            at = start % BANK
-            nc.vector.tensor_copy(
-                x_code[start // BANK][:, at : at + width], word_table[:].indirect(entries(offs_sb, start, width))
-            )
+        deal(nc, w1_bf[:], w1_left[:], 0, P // 2)
+        deal(nc, w1_bf[:], w1_right[:], P // 2, P // 2)
+        x_code = [keep.tile([P, BANK], U32, name=f"x_code{side}", align_bytes=64) for side in range(2)]
+        for side in range(2):
+            nc.vector.tensor_copy(x_code[side][:], word_table[:].indirect(entries(offs_sb, side * BANK, BANK)))
+        w1_plane0 = quantize(w1_bf[:, :H], "w1_plane0")
+        w1_plane1 = quantize(w1_bf[:, H : 2 * H], "w1_plane1")
+        w1_rest = quantize(w1_bf[:, 2 * H :], "w1_rest")
+        w1_q = ((w1_plane0, block(0)), (w1_plane1, block(0)), (w1_rest, block(0)), (w1_rest, block(1)))
 
         y_win = [keep.tile([P, S], F32, name=f"y_win{t}", align_bytes=64) for t in range(PACK)]
-        y_own = [[keep.tile([P, S // 2], F32, name=f"y_own{t}_{half}", align_bytes=64) for half in range(2)] for t in range(PACK)]
+        y_own = [
+            [keep.tile([P, BANK], F32, name=f"y_own{t}_{side}", align_bytes=64) for side in range(2)]
+            for t in range(PACK)
+        ]
         d = [keep.tile([P, S], F32, name=f"d{t}") for t in range(PACK)]
-        c_first = {}
-        c_sum = {}
+        c_first = []
 
         def fine_residual(t):
-            pieces = TOKEN_PIECES if t == 0 else ((0, BANK), (BANK, BANK))
-            first_bank = (0, 3, 5, 7)[t]
-            y_acc = []
-            for piece, (start, width) in enumerate(pieces):
-                acc = psum.tile([P, width], F32, name="acc", tag=f"bank{(first_bank + piece) % 8}")
-                at = start % BANK
-                product(acc[:], w1_q, block(t), x_code[start // BANK][:, at : at + width], x_scale[:, start : start + width])
-                y_acc.append(acc)
-            for acc, (start, width) in zip(y_acc, pieces):
-                nc.scalar.copy(y_win[t][:, start : start + width], acc[:])
-            for acc, (start, width) in zip(y_acc, pieces):
-                at = start % BANK
-                own_copy = nc.vector.tensor_copy if (t, start) == (0, 0) else nc.scalar.copy
-                own_copy(y_own[t][start // BANK][:, at : at + width], acc[:])
-            for start in (0, S // 2):
-                cols = slice(start, start + S // 2)
-                nc.vector.tensor_tensor(
-                    d[t][:, cols], y_win[t][:].indirect(entries(nb_sb, start, S // 2)), y_own[t][start // (S // 2)][:], SUB
-                )
+            y_acc = [psum.tile([P, BANK], F32, name="y_acc", tag=f"bank{2 * t + side}") for side in range(2)]
+            sides = [slice(side * BANK, (side + 1) * BANK) for side in range(2)]
+            for side in range(2):
+                product(y_acc[side][:], *w1_q[t], x_code[side][:], x_scale[:, sides[side]])
+            for side in range(2):
+                nc.scalar.copy(y_win[t][:, sides[side]], y_acc[side][:])
+            for side in range(2):
+                own_copy = nc.vector.tensor_copy if (t, side) == (0, 0) else nc.scalar.copy
+                own_copy(y_own[t][side][:], y_acc[side][:])
+            for side in range(2):
+                gathered = y_win[t][:].indirect(entries(nb_sb, side * BANK, BANK))
+                nc.vector.tensor_tensor(d[t][:, sides[side]], gathered, y_own[t][side][:], SUB)
 
         def coarse_first(t, start, width):
             nc.vector.tensor_copy(c_first[t][:, start : start + width], d[t][:].indirect(entries(c1_sb, start, width)))
 
-        def coarse_sum(half, t):
-            nc.vector.tensor_tensor(
-                c_sum[half][:, t * HALF : (t + 1) * HALF],
-                d[t][:].indirect(entries(c2_sb, half * HALF, HALF)),
-                c_first[t][:, half * HALF : (half + 1) * HALF],
-                ADD,
-            )
-
         for t in range(PACK):
             fine_residual(t)
             if t > 0:
-                c_first[t - 1] = keep.tile([P, V], F32, name="c_first", tag=f"y_own{t}_0", align_bytes=64)
+                c_first.append(keep.tile([P, V], F32, name="c_first", tag=f"y_own{t}_0", align_bytes=64))
                 coarse_first(t - 1, 0, V)
 
         w2_bf = keep.tile([P, PACK * H], BF16, tag="y_win1", align_bytes=64)
-        deal(nc.scalar.copy, w2_bf[:], w2_raw[:], 0, P)
+        deal(nc, w2_bf[:], w2_raw[:], 0, P)
         w2_q = quantize(w2_bf[:], "w2")
         w3_bf = keep.tile([P, PACK * N], BF16, tag="y_win2", align_bytes=64)
         interleave(nc.scalar.copy, w3_bf[:], w3_raw[:])
 
         total = []
         for b in range(TURNED // P):
-            acc = psum.tile([P, N], F32, name="acc", tag=f"bank{4 + b}")
+            turned_acc = psum.tile([P, N], F32, name="turned_acc", tag=f"bank{4 + b}")
             for t in range(PACK):
-                nc.tensor.transpose(acc[:, block(t)], res_head[:, t, block(b)], identity[:])
-            turned = keep.tile([P, N], F32, name=f"res_turned{b}")
-            nc.scalar.copy(turned[:], acc[:])
+                nc.tensor.transpose(turned_acc[:, block(t)], res_head[:, t, block(b)], identity[:])
+            res_turned = keep.tile([P, N], F32, name=f"res_turned{b}")
+            nc.scalar.copy(res_turned[:], turned_acc[:])
             total.append(psum.tile([P, PACK, P], F32, name="total", tag=f"bank{b}"))
             for t in range(PACK):
                 nc.tensor.matmul(
-                    total[b][:, t, :], turned[:, block(t)], identity[:], start=t == 0, stop=False, is_transpose=True
+                    total[b][:, t, :], res_turned[:, block(t)], identity[:], start=t == 0, stop=False, is_transpose=True
                 )
 
-        c_first[PACK - 1] = keep.tile([P, V], F32, name="c_last")
+        c_first.append(keep.tile([P, V], F32, name="c_last"))
         c_both = keep.tile([P, (2 * PACK - 1) * HALF], F32, tag="y_win3", align_bytes=64)
-        c_sum[0] = c_both[:, (PACK - 1) * HALF :]
-        c_sum[1] = c_both[:, : PACK * HALF]
+        c_sum = (c_both[:, (PACK - 1) * HALF :], c_both[:, : PACK * HALF])
+        c_planes = [values.rearrange("p (t c) -> p t c", t=PACK) for values in c_sum]
+
+        def coarse_sum(half, t):
+            gathered = d[t][:].indirect(entries(c2_sb, half * HALF, HALF))
+            first_term = c_first[t][:, half * HALF : (half + 1) * HALF]
+            nc.vector.tensor_tensor(c_sum[half][:, t * HALF : (t + 1) * HALF], gathered, first_term, ADD)
+
         coarse_first(PACK - 1, 0, HALF)
         for t in range(PACK):
             coarse_sum(0, t)
         coarse_first(PACK - 1, HALF, HALF)
 
         h = [keep.tile([P, V], F32, name=f"h{t}") for t in range(PACK)]
-
-        def planes(tile):
-            return tile[:, : PACK * HALF].rearrange("p (t c) -> p t c", t=PACK)
-
         c_bf0 = keep.tile([P, PACK * HALF], BF16, align_bytes=64)
-        interleave(nc.scalar.copy, c_bf0[:], planes(c_sum[0]))
-        coarse_sum(1, 0)
-        coarse_sum(1, 1)
-        coarse_sum(1, 2)
+        interleave(nc.scalar.copy, c_bf0[:], c_planes[0])
+        for t in range(PACK - 1):
+            coarse_sum(1, t)
         c_q0 = quantize(c_bf0[:], "c0")
-        for first in (0, 2):
-            acc = psum.tile([P, 2, HALF], F32, name="acc", tag=f"bank{4 + first // 2}")
-            for t in (first, first + 1):
-                product(acc[:, t - first, :], w2_q, block(t), c_q0[0][:], c_q0[1][:])
-            for t in (first, first + 1):
-                nc.scalar.copy(h[t][:, :HALF], acc[:, t - first, :])
-        coarse_sum(1, 3)
+        for pair in range(2):
+            h_acc = psum.tile([P, 2, HALF], F32, name="h_acc", tag=f"bank{4 + pair}")
+            for e in range(2):
+                product(h_acc[:, e, :], w2_q, block(2 * pair + e), c_q0[0][:], c_q0[1][:])
+            for e in range(2):
+                nc.scalar.copy(h[2 * pair + e][:, :HALF], h_acc[:, e, :])
+        coarse_sum(1, PACK - 1)
         c_bf1 = keep.tile([P, PACK * HALF], BF16, align_bytes=64)
-        interleave(nc.vector.tensor_copy, c_bf1[:], planes(c_sum[1]))
+        interleave(nc.vector.tensor_copy, c_bf1[:], c_planes[1])
         c_q1 = quantize(c_bf1[:], "c1")
         for t in range(PACK):
-            acc = psum.tile([P, HALF], F32, name="acc", tag=f"bank{4 + (t + 2) % 4}")
-            product(acc[:], w2_q, block(t), c_q1[0][:], c_q1[1][:])
-            nc.scalar.copy(h[t][:, HALF:], acc[:])
+            h_acc = psum.tile([P, HALF], F32, name="h_acc", tag=f"bank{4 + (t + 2) % 4}")
+            product(h_acc[:], w2_q, block(t), c_q1[0][:], c_q1[1][:])
+            nc.scalar.copy(h[t][:, HALF:], h_acc[:])
         w3_q = quantize(w3_bf[:], "w3", tag="c_bf1")
 
-        out_rows = out.rearrange("(t p) s -> p t s", p=P)
         last = len(PLACE_PIECES) - 1
-        z_bf = {}
+        z_bf = []
 
         def correct(piece):
             start, width = PLACE_PIECES[piece]
             z = keep.tile([P, PACK, width], F32, name="z", bufs=2)
             for t in range(PACK):
-                nc.vector.tensor_tensor(
-                    z[:, t, :], h[t][:].indirect(entries(up_sb, start, width)), d[t][:, start : start + width], SUB
-                )
-            z_bf[piece] = keep.tile([P, PACK * width], BF16, name=f"z_bf{piece}", align_bytes=64)
+                gathered = h[t][:].indirect(entries(up_sb, start, width))
+                nc.vector.tensor_tensor(z[:, t, :], gathered, d[t][:, start : start + width], SUB)
+            z_bf.append(keep.tile([P, PACK * width], BF16, name=f"z_bf{piece}", align_bytes=64))
             interleave(nc.vector.tensor_copy if piece == last else nc.scalar.copy, z_bf[piece][:], z[:])
 
         def finish_turned(start, width, z_q):
             product_turned = []
             for local in range(width // P):
-                acc = psum.tile([P, N], F32, name="acc", tag=f"bank{4 + local}")
-                product(acc[:], z_q, block(local), w3_q[0][:], w3_q[1][:])
-                product_turned.append(keep.tile([P, N], F32, name="product_turned", bufs=4))
-                nc.scalar.copy(product_turned[local][:], acc[:])
+                out_acc = psum.tile([P, N], F32, name="out_acc", tag=f"bank{4 + local}")
+                product(out_acc[:], z_q, block(local), w3_q[0][:], w3_q[1][:])
+                product_turned.append(keep.tile([P, N], F32, name="product_turned", bufs=TURNED // P))
+                nc.scalar.copy(product_turned[local][:], out_acc[:])
+            result = keep.tile([P, PACK, width], F32, name=f"result{start}")
             for local in range(width // P):
                 b = start // P + local
                 for t in range(PACK):
                     nc.tensor.matmul(
-                        total[b][:, t, :], product_turned[local][:, block(t)], identity[:],
-                        start=False, stop=t == PACK - 1, is_transpose=True,
+                        total[b][:, t, :],
+                        product_turned[local][:, block(t)],
+                        identity[:],
+                        start=False,
+                        stop=t == PACK - 1,
+                        is_transpose=True,
                     )
-                result = keep.tile([P, PACK, P], F32, name=f"result{b}")
-                nc.scalar.copy(result[:], total[b][:])
-                nc.sync.dma_start(out_rows[:, :, block(b)], result[:])
+                nc.scalar.copy(result[:, :, block(local)], total[b][:])
+            nc.sync.dma_start(out_rows[:, :, start : start + width], result[:])
 
         def finish_direct(piece, start, width, z_q):
             share = BANK // width
             for first in range(0, PACK, share):
-                acc = psum.tile([P, share, width], F32, name="acc", tag=f"bank{6 + (piece + first // share) % 2}")
+                out_acc = psum.tile(
+                    [P, share, width], F32, name="out_acc", tag=f"bank{6 + (piece + first // share) % 2}"
+                )
                 for t in range(first, first + share):
-                    product(acc[:, t - first, :], w3_q, block(t), z_q[0][:], z_q[1][:])
+                    product(out_acc[:, t - first, :], w3_q, block(t), z_q[0][:], z_q[1][:])
                 rows = slice(first, first + share)
-                result = keep.tile([P, share, width], F32, name=f"result{piece}_{first}")
+                result = keep.tile([P, share, width], F32, name=f"result{start}_{first}")
                 nc.vector.tensor_tensor(
-                    result[:], acc[:], res_tail[:, rows, start - TURNED : start - TURNED + width], ADD
+                    result[:], out_acc[:], res_tail[:, rows, start - TURNED : start - TURNED + width], ADD
                 )
                 nc.sync.dma_start(out_rows[:, rows, start : start + width], result[:])
 
@@ -274,8 +271,8 @@ def tile_picked_twogrid_none_p_kernel(
             else:
                 finish_direct(piece, start, width, z_q)
 
-        for piece in range(last + 2):
-            if piece <= last:
-                correct(piece)
-            if piece > 0:
-                finish(piece - 1)
+        correct(0)
+        for piece in range(1, last + 1):
+            correct(piece)
+            finish(piece - 1)
+        finish(last)

from contextlib import ExitStack

import concourse.mybir as mybir
from concourse.masks import make_identity

K, T, S, V, H, N = 512, 2048, 1024, 512, 512, 512
FLOPS = 2 * K * H * S + 2 * H * H * V + 2 * H * N * S

F32 = mybir.dt.float32
BF16 = mybir.dt.bfloat16
I32 = mybir.dt.int32
U32 = mybir.dt.uint32
U16 = mybir.dt.uint16
U8 = mybir.dt.uint8
FP8X4 = mybir.dt.float8_e4m3fn_x4
ADD = mybir.AluOpType.add
SUB = mybir.AluOpType.subtract

P = 128
PACK = 4
PER_COL = 16
QUADRANT = 32
BANK = 512
LINE = 4
HALF = V // 2

PLACE_PIECES = ((0, 256), (256, 256), (512, 256), (768, 128), (896, 128))
TURNED = 512


def entries(offsets, start, count):
    return offsets[:, start // PER_COL : (start + count) // PER_COL]


def block(index):
    return slice(index * P, (index + 1) * P)


def interleave(copy, grouped, planes):
    copy(
        out=grouped.rearrange("p (c i t) -> p c t i", i=LINE, t=PACK),
        in_=planes.rearrange("p t (c i) -> p c t i", i=LINE),
    )


def deal(nc, grouped, raw, m0, count):
    nc.scalar.copy(
        out=grouped.rearrange("p (t m j) -> p m t j", t=PACK, j=PACK)[:, m0 : m0 + count],
        in_=raw.rearrange("p j (m t) -> p m t j", t=PACK),
    )


def tile_picked_twogrid_none_p_kernel(
    tc, x_words, x_scales, w1, w2, res, w3, offs, nb, c1, c2, up, out
):
    nc = tc.nc
    with ExitStack() as ctx:
        lists = ctx.enter_context(tc.tile_pool(name="lists", bufs=1))
        keep = ctx.enter_context(tc.tile_pool(name="keep", bufs=1))
        psum = ctx.enter_context(tc.psum_pool(name="psum", bufs=1))

        def quantize(grouped, name, tag=""):
            width = grouped.shape[1] // PACK
            codes = keep.tile([P, width], U32, name=name + "_codes", tag=tag, align_bytes=64)
            scales = keep.tile([P, width], U8, name=name + "_scales", align_bytes=64)
            nc.vector.quantize_mx(out=codes[:].bitcast(FP8X4), scales=scales[:], in_=grouped)
            return codes, scales

        def product(acc, stationary, cols, moving_codes, moving_scales):
            nc.tensor.matmul_mx(
                out=acc,
                lhsT=stationary[0][:, cols].bitcast(FP8X4),
                lhsT_scale=stationary[1][:, cols],
                rhs=moving_codes.bitcast(FP8X4),
                rhs_scale=moving_scales,
                start=True,
                stop=True,
            )

        def load_list(src, name):
            tile = lists.tile(list(src.shape), U16, name=name)
            nc.sync.dma_start(tile[:], src)
            return tile

        scale_table = keep.tile([P, T], U8, align_bytes=64)
        nc.gpsimd.memset(scale_table[:].bitcast(I32), 0)
        offs_sb = load_list(offs, "offs_sb")
        for q in range(P // QUADRANT):
            nc.sync.dma_start(
                scale_table[QUADRANT * q : QUADRANT * q + 4, :].bitcast(I32),
                x_scales[0, 4 * q : 4 * q + 4, :].bitcast(I32),
            )
        w1_rows = w1.rearrange("(p j) c -> p j c", j=PACK)
        w1_left = keep.tile([P, PACK, H // 2], F32)
        nc.sync.dma_start(w1_left[:], w1_rows[:, :, : H // 2])
        word_table = keep.tile([P, T], U32, align_bytes=64)
        nc.sync.dma_start(word_table[:].bitcast(I32), x_words[0].rearrange("p n r -> p (n r)").bitcast(I32))
        w1_right = keep.tile([P, PACK, H // 2], F32)
        nc.sync.dma_start(w1_right[:], w1_rows[:, :, H // 2 :])
        nb_sb = load_list(nb, "nb_sb")
        c1_sb = load_list(c1, "c1_sb")
        c2_sb = load_list(c2, "c2_sb")
        up_sb = load_list(up, "up_sb")
        w2_raw = keep.tile([P, PACK, H], F32)
        nc.sync.dma_start(w2_raw[:], w2.rearrange("(p j) c -> p j c", j=PACK))
        res_rows = res.rearrange("(t p) s -> p t s", p=P)
        out_rows = out.rearrange("(t p) s -> p t s", p=P)
        res_head = keep.tile([P, PACK, TURNED], F32)
        nc.sync.dma_start(res_head[:], res_rows[:, :, :TURNED])
        w3_raw = keep.tile([P, PACK, N], F32)
        nc.sync.dma_start(w3_raw[:], w3.rearrange("(p j) c -> p j c", j=PACK))
        res_tail = keep.tile([P, PACK, S - TURNED], F32)
        nc.sync.dma_start(res_tail[:], res_rows[:, :, TURNED:])
        identity = keep.tile([P, P], F32)
        make_identity(nc, identity[:])

        x_scale = keep.tile([P, S], U8, align_bytes=64)
        nc.vector.tensor_copy(x_scale[:], scale_table[:].indirect(offs_sb[:]))
        w1_bf = keep.tile([P, PACK * H], BF16, align_bytes=64)
        deal(nc, w1_bf[:], w1_left[:], 0, P // 2)
        deal(nc, w1_bf[:], w1_right[:], P // 2, P // 2)
        x_code = [keep.tile([P, BANK], U32, name=f"x_code{side}", align_bytes=64) for side in range(2)]
        for side in range(2):
            nc.vector.tensor_copy(x_code[side][:], word_table[:].indirect(entries(offs_sb, side * BANK, BANK)))
        w1_plane0 = quantize(w1_bf[:, :H], "w1_plane0")
        w1_plane1 = quantize(w1_bf[:, H : 2 * H], "w1_plane1")
        w1_rest = quantize(w1_bf[:, 2 * H :], "w1_rest")
        w1_q = ((w1_plane0, block(0)), (w1_plane1, block(0)), (w1_rest, block(0)), (w1_rest, block(1)))

        y_win = [keep.tile([P, S], F32, name=f"y_win{t}", align_bytes=64) for t in range(PACK)]
        y_own = [
            [keep.tile([P, BANK], F32, name=f"y_own{t}_{side}", align_bytes=64) for side in range(2)]
            for t in range(PACK)
        ]
        d = [keep.tile([P, S], F32, name=f"d{t}") for t in range(PACK)]
        c_first = []

        def fine_residual(t):
            y_acc = [psum.tile([P, BANK], F32, name="y_acc", tag=f"bank{2 * t + side}") for side in range(2)]
            sides = [slice(side * BANK, (side + 1) * BANK) for side in range(2)]
            for side in range(2):
                product(y_acc[side][:], *w1_q[t], x_code[side][:], x_scale[:, sides[side]])
            for side in range(2):
                nc.scalar.copy(y_win[t][:, sides[side]], y_acc[side][:])
            for side in range(2):
                own_copy = nc.vector.tensor_copy if (t, side) == (0, 0) else nc.scalar.copy
                own_copy(y_own[t][side][:], y_acc[side][:])
            for side in range(2):
                gathered = y_win[t][:].indirect(entries(nb_sb, side * BANK, BANK))
                nc.vector.tensor_tensor(d[t][:, sides[side]], gathered, y_own[t][side][:], SUB)

        def coarse_first(t, start, width):
            nc.vector.tensor_copy(c_first[t][:, start : start + width], d[t][:].indirect(entries(c1_sb, start, width)))

        for t in range(PACK):
            fine_residual(t)
            if t > 0:
                c_first.append(keep.tile([P, V], F32, name="c_first", tag=f"y_own{t}_0", align_bytes=64))
                coarse_first(t - 1, 0, V)

        w2_bf = keep.tile([P, PACK * H], BF16, tag="y_win1", align_bytes=64)
        deal(nc, w2_bf[:], w2_raw[:], 0, P)
        w2_q = quantize(w2_bf[:], "w2")
        w3_bf = keep.tile([P, PACK * N], BF16, tag="y_win2", align_bytes=64)
        interleave(nc.scalar.copy, w3_bf[:], w3_raw[:])

        total = []
        for b in range(TURNED // P):
            turned_acc = psum.tile([P, N], F32, name="turned_acc", tag=f"bank{4 + b}")
            for t in range(PACK):
                nc.tensor.transpose(turned_acc[:, block(t)], res_head[:, t, block(b)], identity[:])
            res_turned = keep.tile([P, N], F32, name=f"res_turned{b}")
            nc.scalar.copy(res_turned[:], turned_acc[:])
            total.append(psum.tile([P, PACK, P], F32, name="total", tag=f"bank{b}"))
            for t in range(PACK):
                nc.tensor.matmul(
                    total[b][:, t, :], res_turned[:, block(t)], identity[:], start=t == 0, stop=False, is_transpose=True
                )

        c_first.append(keep.tile([P, V], F32, name="c_last"))
        c_both = keep.tile([P, (2 * PACK - 1) * HALF], F32, tag="y_win3", align_bytes=64)
        c_sum = (c_both[:, (PACK - 1) * HALF :], c_both[:, : PACK * HALF])
        c_planes = [values.rearrange("p (t c) -> p t c", t=PACK) for values in c_sum]

        def coarse_sum(half, t):
            gathered = d[t][:].indirect(entries(c2_sb, half * HALF, HALF))
            first_term = c_first[t][:, half * HALF : (half + 1) * HALF]
            nc.vector.tensor_tensor(c_sum[half][:, t * HALF : (t + 1) * HALF], gathered, first_term, ADD)

        coarse_first(PACK - 1, 0, HALF)
        for t in range(PACK):
            coarse_sum(0, t)
        coarse_first(PACK - 1, HALF, HALF)

        h = [keep.tile([P, V], F32, name=f"h{t}") for t in range(PACK)]
        c_bf0 = keep.tile([P, PACK * HALF], BF16, align_bytes=64)
        interleave(nc.scalar.copy, c_bf0[:], c_planes[0])
        for t in range(PACK - 1):
            coarse_sum(1, t)
        c_q0 = quantize(c_bf0[:], "c0")
        for pair in range(2):
            h_acc = psum.tile([P, 2, HALF], F32, name="h_acc", tag=f"bank{4 + pair}")
            for e in range(2):
                product(h_acc[:, e, :], w2_q, block(2 * pair + e), c_q0[0][:], c_q0[1][:])
            for e in range(2):
                nc.scalar.copy(h[2 * pair + e][:, :HALF], h_acc[:, e, :])
        coarse_sum(1, PACK - 1)
        c_bf1 = keep.tile([P, PACK * HALF], BF16, align_bytes=64)
        interleave(nc.vector.tensor_copy, c_bf1[:], c_planes[1])
        c_q1 = quantize(c_bf1[:], "c1")
        for t in range(PACK):
            h_acc = psum.tile([P, HALF], F32, name="h_acc", tag=f"bank{4 + (t + 2) % 4}")
            product(h_acc[:], w2_q, block(t), c_q1[0][:], c_q1[1][:])
            nc.scalar.copy(h[t][:, HALF:], h_acc[:])
        w3_q = quantize(w3_bf[:], "w3", tag="c_bf1")

        last = len(PLACE_PIECES) - 1
        z_bf = []

        def correct(piece):
            start, width = PLACE_PIECES[piece]
            z = keep.tile([P, PACK, width], F32, name="z", bufs=2)
            for t in range(PACK):
                gathered = h[t][:].indirect(entries(up_sb, start, width))
                nc.vector.tensor_tensor(z[:, t, :], gathered, d[t][:, start : start + width], SUB)
            z_bf.append(keep.tile([P, PACK * width], BF16, name=f"z_bf{piece}", align_bytes=64))
            interleave(nc.vector.tensor_copy if piece == last else nc.scalar.copy, z_bf[piece][:], z[:])

        def finish_turned(start, width, z_q):
            product_turned = []
            for local in range(width // P):
                out_acc = psum.tile([P, N], F32, name="out_acc", tag=f"bank{4 + local}")
                product(out_acc[:], z_q, block(local), w3_q[0][:], w3_q[1][:])
                product_turned.append(keep.tile([P, N], F32, name="product_turned", bufs=TURNED // P))
                nc.scalar.copy(product_turned[local][:], out_acc[:])
            result = keep.tile([P, PACK, width], F32, name=f"result{start}")
            for local in range(width // P):
                b = start // P + local
                for t in range(PACK):
                    nc.tensor.matmul(
                        total[b][:, t, :],
                        product_turned[local][:, block(t)],
                        identity[:],
                        start=False,
                        stop=t == PACK - 1,
                        is_transpose=True,
                    )
                nc.scalar.copy(result[:, :, block(local)], total[b][:])
            nc.sync.dma_start(out_rows[:, :, start : start + width], result[:])

        def finish_direct(piece, start, width, z_q):
            share = BANK // width
            for first in range(0, PACK, share):
                out_acc = psum.tile(
                    [P, share, width], F32, name="out_acc", tag=f"bank{6 + (piece + first // share) % 2}"
                )
                for t in range(first, first + share):
                    product(out_acc[:, t - first, :], w3_q, block(t), z_q[0][:], z_q[1][:])
                rows = slice(first, first + share)
                result = keep.tile([P, share, width], F32, name=f"result{start}_{first}")
                nc.vector.tensor_tensor(
                    result[:], out_acc[:], res_tail[:, rows, start - TURNED : start - TURNED + width], ADD
                )
                nc.sync.dma_start(out_rows[:, rows, start : start + width], result[:])

        def finish(piece):
            start, width = PLACE_PIECES[piece]
            z_q = quantize(z_bf[piece][:], f"z{piece}")
            if start < TURNED:
                finish_turned(start, width, z_q)
            else:
                finish_direct(piece, start, width, z_q)

        correct(0)
        for piece in range(1, last + 1):
            correct(piece)
            finish(piece - 1)
        finish(last)
